import numpy as np
import ml_dtypes


def mxq(x, axis, fmt="e4m3"):
    dtype, down = {"e4m3": (ml_dtypes.float8_e4m3fn, 7), "e5m2": (ml_dtypes.float8_e5m2, 14)}[fmt]
    v = np.moveaxis(np.asarray(x, np.float32).astype(ml_dtypes.bfloat16).astype(np.float64), axis, -1)
    blocks = v.reshape(v.shape[:-1] + (-1, 32))
    amax = np.abs(blocks).max(-1, keepdims=True)
    byte = np.maximum(np.where(amax > 0, np.frexp(amax)[1] - 1 + 127, 0) - down, 1)
    scale = np.exp2(byte - 127.0)
    codes = (blocks / scale).astype(np.float32).astype(dtype).astype(np.float64)
    return np.moveaxis((codes * scale).reshape(v.shape), -1, axis)


WIDE = False


def mx_kscale(k):
    if not WIDE:
        return np.ones(k)
    levels = np.array([10, -10, 5, -5, 0])
    if k % 512:
        return np.exp2(np.random.permutation(np.resize(levels, k // 32))).repeat(32)
    a = np.empty((k // 512, 16))
    for p in range(k // 512):
        a[p, :8] = np.random.permutation(np.resize(levels, 8))
        for g in range(8):
            far = levels[np.abs(levels - a[p, g]) >= 10]
            a[p, g + 8] = far[np.random.randint(len(far))]
    return np.exp2(a.ravel()).repeat(32)


def f64(x):
    return np.asarray(x).astype(np.float64)


def striped(idx):
    return np.tile(idx.reshape(-1, 16).T, (8, 1)).astype(np.uint16)


def unstriped(offs):
    return offs[:16].T.reshape(-1).astype(np.int64)


E2M1 = np.array([0.0, 0.5, 1.0, 1.5, 2.0, 3.0, 4.0, 6.0, -0.0, -0.5, -1.0, -1.5, -2.0, -3.0, -4.0, -6.0])


def pack_weight(w, fmt):
    k, n = w.shape
    w = f64(np.asarray(w, np.float32).astype(ml_dtypes.bfloat16)).reshape(k // 32, 32, n)
    amax = np.abs(w).max(1)
    if fmt == "e4m3":
        byte = np.frexp(amax)[1] - 1 + 127 - 7
    else:
        mant, ex = np.frexp(amax / 6.0)
        byte = np.where(mant > 0.5, ex, ex - 1) + 127
    byte = np.clip(np.where(amax > 0, byte, 1), 1, 254)
    scaled = (w * np.exp2(127.0 - byte)[:, None, :]).reshape(k, n).astype(np.float32)
    by_word = np.ascontiguousarray(scaled.reshape(k // 512, 128, 4, n).transpose(0, 1, 3, 2))
    if fmt == "e4m3":
        words = by_word.astype(ml_dtypes.float8_e4m3fn).view(np.uint8)
    else:
        c = by_word.astype(ml_dtypes.float4_e2m1fn).view(np.uint8) & 0xF
        words = (c[..., 0::2] | (c[..., 1::2] << 4)).reshape(k // 512, 128, 2 * n)
    return np.ascontiguousarray(words), np.ascontiguousarray(byte.astype(np.uint8).reshape(k // 512, 16, n))


def unpack_weight(words, scales, fmt):
    g, _, n = scales.shape
    words = np.ascontiguousarray(words).reshape(g, 128, n, -1)
    if fmt == "e4m3":
        vals = words.view(ml_dtypes.float8_e4m3fn).astype(np.float64)
    else:
        nib = np.empty((g, 128, n, 4), np.uint8)
        nib[..., 0::2] = words & 0xF
        nib[..., 1::2] = words >> 4
        vals = E2M1[nib]
    vals = vals * np.repeat(np.exp2(scales.astype(np.float64) - 127.0), 8, axis=1)[..., None]
    return vals.transpose(0, 1, 3, 2).reshape(g * 512, n)


def gelu(v):
    return 0.5 * v * (1.0 + np.tanh(np.sqrt(2.0 / np.pi) * (v + 0.044715 * v**3)))


K, T, S, H, T3, S2, P = 1024, 2048, 1024, 512, 2048, 512, 512

def setup_inputs():
    n = np.random.standard_normal
    ks = mx_kscale(K)[:, None]
    u = mx_kscale(H)[:, None]
    tab_words, tab_scales = pack_weight(n((K, T)) * ks, "e4m3")
    tab2_words, tab2_scales = pack_weight(n((H, T3)) / np.sqrt(H) / u, "e4m3")
    w2_words, w2_scales = pack_weight(1.2 * n((K, H)) / np.sqrt(K) / ks, "e2m1")
    w4_words, w4_scales = pack_weight(n((H, S2)) / np.sqrt(H) / u, "e4m3")
    return {
        "tab_words": tab_words, "tab_scales": tab_scales,
        "offs": striped(np.random.permutation(T)[:S]),
        "tab2_words": tab2_words, "tab2_scales": tab2_scales,
        "offs2": striped(np.random.permutation(T3)[:S2]),
        "pos1": striped(np.random.permutation(S)[:P]),
        "pos2": striped(np.random.permutation(S)[:P]),
        "w1": (0.7 * n((K, H)) / np.sqrt(K) / ks * u.T).astype(np.float32),
        "b1": (0.3 * n(H) * u[:, 0]).astype(np.float32),
        "w2_words": w2_words, "w2_scales": w2_scales,
        "b2": (0.5 * n(H)).astype(np.float32),
        "gain": (np.random.uniform(0.6, 1.6, H) * u[:, 0]).astype(np.float32),
        "w3": (1.3 * n((H, S2)) / np.sqrt(H) / u).astype(np.float32),
        "w4_words": w4_words, "w4_scales": w4_scales,
        "steep": np.random.uniform(1, 3, S2).astype(np.float32),
        "share": np.random.uniform(0.1, 0.5, S2).astype(np.float32),
        "lam": (np.random.uniform(0.7, 2.5, S2) * np.sign(n(S2))).astype(np.float32),
    }

def reference(tab_words, tab_scales, offs, tab2_words, tab2_scales, offs2, pos1, pos2,
              w1, b1, w2_words, w2_scales, b2, gain, w3, w4_words, w4_scales, steep, share, lam):
    v = unpack_weight(tab_words, tab_scales, "e4m3")[:, unstriped(offs)]
    v2 = unpack_weight(tab2_words, tab2_scales, "e4m3")[:, unstriped(offs2)]
    w2 = unpack_weight(w2_words, w2_scales, "e2m1")
    w4 = unpack_weight(w4_words, w4_scales, "e4m3")
    h = (mxq(f64(w1), 0, "e4m3").T @ v) + f64(b1)[:, None]
    z = (w2.T @ v) + f64(b2)[:, None]
    g = 0.5 * z * (1.0 + np.tanh(np.sqrt(2.0 / np.pi) * (z + 0.044715 * z ** 3)))
    g = f64(gain)[:, None] * g
    hq = mxq(h, 0, "e4m3")
    gq = mxq(g, 0, "e4m3")
    e = v2.T @ hq
    d = mxq(f64(w3), 0, "e4m3").T @ hq + w4.T @ gq
    top = e.max(axis=1)
    a = 1.0 / (1.0 + np.exp(-f64(steep)[:, None] * (e[:, unstriped(pos1)] - f64(share)[:, None] * top[:, None])))
    c = d[:, unstriped(pos2)]
    return f64(lam)[:, None] * (a * c)

@@ -1,0 +1,262 @@
+from contextlib import ExitStack
+
+import concourse.mybir as mybir
+
+K, T, S, H, T3, S2, NP = 1024, 2048, 1024, 512, 2048, 512, 512
+FLOPS = 2 * (2 * K * H * S + 3 * H * S2 * S)
+
+F32 = mybir.dt.float32
+BF16 = mybir.dt.bfloat16
+I32 = mybir.dt.int32
+U32 = mybir.dt.uint32
+U16 = mybir.dt.uint16
+U8 = mybir.dt.uint8
+FP8X4 = mybir.dt.float8_e4m3fn_x4
+FP4X4 = mybir.dt.float4_e2m1fn_x4
+ACT = mybir.ActivationFunctionType
+ALU = mybir.AluOpType
+
+P = 128
+PACK = 4
+N = 512
+PASSES = 2
+HALVES = 2
+QUADS = 4
+MT = 4
+
+
+def tile_list_framework_pore_scores_kernel(
+    tc, tab_words, tab_scales, offs, tab2_words, tab2_scales, offs2, pos1, pos2,
+    w1, b1, w2_words, w2_scales, b2, gain, w3, w4_words, w4_scales, steep, share, lam, out,
+):
+    nc = tc.nc
+    with ExitStack() as ctx:
+        lists = ctx.enter_context(tc.tile_pool(name="lists", bufs=1))
+        keep = ctx.enter_context(tc.tile_pool(name="keep", bufs=1))
+        psum = ctx.enter_context(tc.psum_pool(name="psum", bufs=8))
+
+        def held(name, shape, dtype):
+            return keep.tile(shape, dtype, name=name, align_bytes=64)
+
+        def load_words(dst, words):
+            nc.sync.dma_start(out=dst[:], in_=words.rearrange("p n i -> p (n i)").bitcast(I32))
+
+        def load_list(name, src):
+            t = lists.tile(list(src.shape), U16, name=name)
+            nc.sync.dma_start(t[:], src)
+            return t
+
+        def load_plane(dst, scales):
+            for q in range(QUADS):
+                nc.sync.dma_start(out=dst[32 * q : 32 * q + 4, :].bitcast(I32), in_=scales[4 * q : 4 * q + 4, :].bitcast(I32))
+
+        def mm(acc, lhs, lhs_s, rhs, rhs_s, start, stop, fmt=FP8X4):
+            nc.tensor.matmul_mx(out=acc, lhsT=lhs.bitcast(fmt), lhsT_scale=lhs_s, rhs=rhs.bitcast(FP8X4), rhs_scale=rhs_s, start=start, stop=stop)
+
+        def quantize(name, grouped):
+            codes = held(name + "_codes", [P, N], I32)
+            plane = held(name + "_plane", [P, N], U8)
+            nc.vector.quantize_mx(out=codes[:].bitcast(FP8X4), scales=plane[:], in_=grouped[:])
+            return codes, plane
+
+        tab_plane = held("tab_plane", [P, T], U8)
+        nc.vector.memset(tab_plane[:].bitcast(I32), 0)
+        w2_plane_raw = held("w2_plane_raw", [P, PASSES * H], U8)
+        nc.gpsimd.memset(w2_plane_raw[:].bitcast(I32), 0)
+        v_plane1 = held("v_plane1", [P, S], U8)
+        nc.gpsimd.memset(v_plane1[:].bitcast(I32), 0)
+        tab2_plane = held("tab2_plane", [P, T3], U8)
+        nc.gpsimd.memset(tab2_plane[:].bitcast(I32), 0)
+        w4_plane = held("w4_plane", [P, S2], U8)
+        nc.gpsimd.memset(w4_plane[:].bitcast(I32), 0)
+
+        offs_t = load_list("offs_t", offs)
+        tab_rows = held("tab_rows", [P, T // 4], I32)
+        for q in range(QUADS):
+            nc.sync.dma_start(out=tab_rows[32 * q : 32 * q + 8, :], in_=tab_scales[:, 4 * q : 4 * q + 4, :].bitcast(I32))
+        tab = [held("tab%d" % a, [P, T], I32) for a in range(PASSES)]
+        load_words(tab[0], tab_words[0])
+        w2_both = held("w2_both", [P, PASSES, 2 * H // 4], I32)
+        nc.sync.dma_start(out=w2_both[:], in_=w2_words.rearrange("a p n -> p a n").bitcast(I32))
+        w1_raw = [held("w1_raw%d" % a, [P, PACK, H], F32) for a in range(PASSES)]
+        nc.sync.dma_start(out=w1_raw[0][:], in_=w1[0:512, :].rearrange("(p j) c -> p j c", j=PACK))
+        for q in range(QUADS):
+            nc.sync.dma_start(
+                out=w2_plane_raw[32 * q : 32 * q + 4, :].bitcast(I32).rearrange("r (a n) -> r a n", a=PASSES),
+                in_=w2_scales[:, 4 * q : 4 * q + 4, :].rearrange("a r n -> r a n").bitcast(I32),
+            )
+        load_words(tab[1], tab_words[1])
+        offs2_t = load_list("offs2_t", offs2)
+        b2_t = held("b2_t", [P, PACK], F32)
+        nc.sync.dma_start(out=b2_t[:], in_=b2.rearrange("(p t) -> p t", t=PACK))
+        nc.sync.dma_start(out=w1_raw[1][:], in_=w1[512:1024, :].rearrange("(p j) c -> p j c", j=PACK))
+        load_plane(tab2_plane, tab2_scales[0])
+        gain_t = held("gain_t", [P, PACK], F32)
+        nc.sync.dma_start(out=gain_t[:], in_=gain.rearrange("(p t) -> p t", t=PACK))
+        tab2 = held("tab2", [P, T3], I32)
+        load_words(tab2, tab2_words[0])
+        b1_t = held("b1_t", [P, PACK], F32)
+        nc.sync.dma_start(out=b1_t[:], in_=b1.rearrange("(p t) -> p t", t=PACK))
+        w3_raw = held("w3_raw", [P, PACK, S2], F32)
+        nc.sync.dma_start(out=w3_raw[:], in_=w3.rearrange("(p j) c -> p j c", j=PACK))
+        w4 = held("w4", [P, S2], I32)
+        load_words(w4, w4_words[0])
+        load_plane(w4_plane, w4_scales[0])
+        pos1_t = load_list("pos1_t", pos1)
+        pos2_t = load_list("pos2_t", pos2)
+        steep_t = held("steep_t", [P, MT], F32)
+        share_t = held("share_t", [P, MT], F32)
+        lam_t = held("lam_t", [P, MT], F32)
+        with nc.allow_non_contiguous_dma(reason="one value for each output row"):
+            for dst, src in ((steep_t, steep), (share_t, share), (lam_t, lam)):
+                nc.sync.dma_start(out=dst[:], in_=src.rearrange("(t p) -> p t", p=P))
+
+        for q in range(QUADS):
+            rows = slice(32 * q, 32 * q + 8)
+            nc.vector.tensor_copy(out=tab_plane[rows, :].bitcast(I32), in_=tab_rows[rows, :])
+        v_plane0 = held("v_plane0", [P, S], U8)
+        nc.vector.tensor_copy(out=v_plane0[:], in_=tab_plane[:].indirect(offs_t[:]))
+        for q in range(QUADS):
+            nc.scalar.dma_start(out=v_plane1[32 * q : 32 * q + 4, :].bitcast(I32), in_=v_plane0[32 * q + 4 : 32 * q + 8, :].bitcast(I32))
+        v_plane = [v_plane0, v_plane1]
+        v = [[held("v%d_%d" % (a, u), [P, N], I32) for u in range(HALVES)] for a in range(PASSES)]
+
+        def gather_v(a):
+            for u in range(HALVES):
+                nc.vector.tensor_copy(out=v[a][u][:].bitcast(U32), in_=tab[a][:].bitcast(U32).indirect(offs_t[:, 32 * u : 32 * (u + 1)]))
+
+        gather_v(0)
+
+        w2 = held("w2", [P, PASSES, 2 * H], U8)
+        nc.scalar.copy(
+            out=w2[:].bitcast(U16).rearrange("p a (t m) -> p a t m", t=PACK),
+            in_=w2_both[:].bitcast(U16).rearrange("p a (m t) -> p a t m", t=PACK),
+        )
+        w2_plane = held("w2_plane", [P, PASSES * H], U8)
+        nc.vector.tensor_copy(
+            out=w2_plane[:].rearrange("p (a t m) -> p a t m", a=PASSES, t=PACK),
+            in_=w2_plane_raw[:].rearrange("p (a m t) -> p a t m", a=PASSES, t=PACK),
+        )
+
+        def group_w1(a, copy):
+            grouped = held("w1_grouped%d" % a, [P, PACK * H], BF16)
+            copy(
+                out=grouped[:].rearrange("p (t m j) -> p m j t", t=PACK, j=PACK),
+                in_=w1_raw[a][:].rearrange("p j (m t) -> p m j t", t=PACK),
+            )
+            return grouped
+
+        w1_grouped0 = group_w1(0, nc.scalar.copy)
+        v2_plane = held("v2_plane", [P, S2], U8)
+        nc.vector.tensor_copy(out=v2_plane[:], in_=tab2_plane[:].indirect(offs2_t[:]))
+        gather_v(1)
+        w1q = [quantize("w1q0", w1_grouped0)]
+
+        bent = [held("bent%d" % u, [P, PACK, N], F32) for u in range(HALVES)]
+        for u in range(HALVES):
+            for t in range(PACK):
+                acc = psum.tile([P, N], F32, name="acc")
+                for a in range(PASSES):
+                    mm(acc[:], w2[:, a, 256 * t : 256 * (t + 1)], w2_plane[:, a * H + P * t : a * H + P * (t + 1)],
+                       v[a][u][:], v_plane[a][:, N * u : N * (u + 1)], a == 0, a == PASSES - 1, FP4X4)
+                nc.scalar.activation(out=bent[u][:, t, :], in_=acc[:], func=ACT.Gelu_apprx_tanh, bias=b2_t[:, t : t + 1])
+
+        w1q.append(quantize("w1q1", group_w1(1, nc.vector.tensor_copy)))
+
+        lin = [held("lin%d" % u, [P, PACK, N], BF16) for u in range(HALVES)]
+
+        def linear(u):
+            for t in range(PACK):
+                acc = psum.tile([P, N], F32, name="acc")
+                for a in range(PASSES):
+                    mm(acc[:], w1q[a][0][:, P * t : P * (t + 1)], w1q[a][1][:, P * t : P * (t + 1)],
+                       v[a][u][:], v_plane[a][:, N * u : N * (u + 1)], a == 0, a == PASSES - 1)
+                nc.scalar.activation(out=lin[u][:, t, :], in_=acc[:], func=ACT.Identity, bias=b1_t[:, t : t + 1])
+
+        def group_g(u):
+            grouped = held("g_grouped%d" % u, [P, PACK * N], BF16)
+            nc.vector.tensor_tensor(
+                out=grouped[:].rearrange("p (c i t) -> p c t i", i=4, t=PACK),
+                in0=bent[u][:].rearrange("p t (c i) -> p c t i", i=4),
+                in1=gain_t[:].unsqueeze(1).unsqueeze(3).to_broadcast([P, N // 4, PACK, 4]),
+                op=ALU.mult,
+            )
+            return grouped
+
+        def group_h(u):
+            grouped = held("h_grouped%d" % u, [P, PACK * N], BF16)
+            nc.vector.tensor_copy(
+                out=grouped[:].rearrange("p (c i t) -> p c t i", i=4, t=PACK),
+                in_=lin[u][:].rearrange("p t (c i) -> p c t i", i=4),
+            )
+            return grouped
+
+        linear(0)
+        g_grouped0 = group_g(0)
+        v2 = held("v2", [P, S2], I32)
+        nc.vector.tensor_copy(out=v2[:].bitcast(U32), in_=tab2[:].bitcast(U32).indirect(offs2_t[:]))
+        gq = [quantize("gq0", g_grouped0)]
+        w3_grouped = held("w3_grouped", [P, PACK * S2], BF16)
+        nc.scalar.copy(
+            out=w3_grouped[:].rearrange("p (c i j) -> p c j i", i=4, j=PACK),
+            in_=w3_raw[:].rearrange("p j (c i) -> p c j i", i=4),
+        )
+        linear(1)
+        h_grouped0 = group_h(0)
+        pull = held("pull", [P, MT], F32)
+        nc.vector.scalar_tensor_tensor(out=pull[:], in0=steep_t[:], scalar=-1.0, in1=share_t[:], op0=ALU.mult, op1=ALU.mult)
+        hq = [quantize("hq0", h_grouped0)]
+        g_grouped1 = group_g(1)
+        w3q = quantize("w3q", w3_grouped)
+        gq.append(quantize("gq1", g_grouped1))
+
+        tops = held("tops", [P, MT * HALVES], F32)
+        shift = held("shift", [P, MT], F32)
+        e = [held("e%d" % m, [P, S], F32) for m in range(MT)]
+        dm = [held("d%d" % m, [P, S], F32) for m in range(MT)]
+        gates = [held("gate%d" % m, [P, NP], F32) for m in range(MT)]
+
+        def score(m, u):
+            cols = slice(P * m, P * (m + 1))
+            acc = psum.tile([P, N], F32, name="acc")
+            mm(acc[:], v2[:, cols], v2_plane[:, cols], hq[u][0][:], hq[u][1][:], True, True)
+            nc.vector.tensor_scalar(
+                out=e[m][:, N * u : N * (u + 1)], in0=acc[:], scalar1=1.0, scalar2=None, op0=ALU.mult, op1=ALU.max,
+                accum_out=tops[:, HALVES * m + u : HALVES * m + u + 1],
+            )
+
+        def look(m):
+            nc.vector.tensor_scalar(
+                out=shift[:, m : m + 1], in0=tops[:, HALVES * m : HALVES * m + 1], scalar1=tops[:, HALVES * m + 1 : HALVES * m + 2],
+                scalar2=pull[:, m : m + 1], op0=ALU.max, op1=ALU.mult,
+            )
+            nc.scalar.activation(out=gates[m][:], in_=e[m][:].indirect(pos1_t[:]), func=ACT.Sigmoid, bias=shift[:, m : m + 1], scale=steep_t[:, m : m + 1])
+
+        def reading(m, u):
+            cols = slice(P * m, P * (m + 1))
+            acc = psum.tile([P, N], F32, name="acc")
+            mm(acc[:], w3q[0][:, cols], w3q[1][:, cols], hq[u][0][:], hq[u][1][:], True, False)
+            mm(acc[:], w4[:, cols], w4_plane[:, cols], gq[u][0][:], gq[u][1][:], False, True)
+            nc.scalar.copy(out=dm[m][:, N * u : N * (u + 1)], in_=acc[:])
+
+        def finish(m):
+            weight = held("weight%d" % m, [P, NP], F32)
+            nc.vector.tensor_scalar(out=weight[:], in0=gates[m][:], scalar1=lam_t[:, m : m + 1], scalar2=None, op0=ALU.mult)
+            res = held("res%d" % m, [P, NP], F32)
+            nc.vector.tensor_tensor(out=res[:], in0=dm[m][:].indirect(pos2_t[:]), in1=weight[:], op=ALU.mult)
+            nc.sync.dma_start(out=out[P * m : P * (m + 1), :], in_=res[:])
+
+        for m in range(MT):
+            reading(m, 0)
+        h_grouped1 = group_h(1)
+        score(0, 0)
+        hq.append(quantize("hq1", h_grouped1))
+        score(1, 0)
+        for m in range(MT):
+            if m >= 2:
+                score(m, 0)
+            score(m, 1)
+            look(m)
+            reading(m, 1)
+        for m in range(MT):
+            finish(m)

@@ -1,6 +1,7 @@
 from contextlib import ExitStack
 
 import concourse.mybir as mybir
+from concourse.masks import make_identity
 
 K, T, S, H, T3, S2, NP = 1024, 2048, 1024, 512, 2048, 512, 512
 FLOPS = 2 * (2 * K * H * S + 3 * H * S2 * S)
@@ -33,10 +34,13 @@ def tile_list_framework_pore_scores_kernel(
     with ExitStack() as ctx:
         lists = ctx.enter_context(tc.tile_pool(name="lists", bufs=1))
         keep = ctx.enter_context(tc.tile_pool(name="keep", bufs=1))
-        psum = ctx.enter_context(tc.psum_pool(name="psum", bufs=8))
+        psum = ctx.enter_context(tc.psum_pool(name="psum", bufs=1))
 
         def held(name, shape, dtype):
             return keep.tile(shape, dtype, name=name, align_bytes=64)
+
+        def bank(b):
+            return psum.tile([P, N], F32, name="bank%d" % b)
 
         def load_words(dst, words):
             nc.sync.dma_start(out=dst[:], in_=words.rearrange("p n i -> p (n i)").bitcast(I32))
@@ -60,7 +64,7 @@ def tile_list_framework_pore_scores_kernel(
             return codes, plane
 
         tab_plane = held("tab_plane", [P, T], U8)
-        nc.vector.memset(tab_plane[:].bitcast(I32), 0)
+        nc.gpsimd.memset(tab_plane[:].bitcast(I32), 0)
         w2_plane_raw = held("w2_plane_raw", [P, PASSES * H], U8)
         nc.gpsimd.memset(w2_plane_raw[:].bitcast(I32), 0)
         v_plane1 = held("v_plane1", [P, S], U8)
@@ -70,33 +74,41 @@ def tile_list_framework_pore_scores_kernel(
         w4_plane = held("w4_plane", [P, S2], U8)
         nc.gpsimd.memset(w4_plane[:].bitcast(I32), 0)
 
+        ident = held("ident", [P, P], F32)
+        make_identity(nc, ident[:])
+        row_vecs = held("row_vecs", [P, P], F32)
+        nc.gpsimd.memset(row_vecs[:], 0.0)
+        for i, vec in enumerate((steep, share, lam)):
+            nc.gpsimd.dma_start(out=row_vecs[MT * i : MT * (i + 1), :], in_=vec.rearrange("(t p) -> t p", p=P))
+
+        def load_column(name, vec):
+            t = held(name, [P, PACK], F32)
+            nc.sync.dma_start(out=t[:], in_=vec.rearrange("(p t) -> p t", t=PACK))
+            return t
+
         offs_t = load_list("offs_t", offs)
-        tab_rows = held("tab_rows", [P, T // 4], I32)
-        for q in range(QUADS):
-            nc.sync.dma_start(out=tab_rows[32 * q : 32 * q + 8, :], in_=tab_scales[:, 4 * q : 4 * q + 4, :].bitcast(I32))
-        tab = [held("tab%d" % a, [P, T], I32) for a in range(PASSES)]
-        load_words(tab[0], tab_words[0])
         w2_both = held("w2_both", [P, PASSES, 2 * H // 4], I32)
         nc.sync.dma_start(out=w2_both[:], in_=w2_words.rearrange("a p n -> p a n").bitcast(I32))
-        w1_raw = [held("w1_raw%d" % a, [P, PACK, H], F32) for a in range(PASSES)]
-        nc.sync.dma_start(out=w1_raw[0][:], in_=w1[0:512, :].rearrange("(p j) c -> p j c", j=PACK))
+        offs2_t = load_list("offs2_t", offs2)
+        for q in range(QUADS):
+            nc.sync.dma_start(out=tab_plane[32 * q : 32 * q + 8, :].bitcast(I32), in_=tab_scales[:, 4 * q : 4 * q + 4, :].bitcast(I32))
+        tab = [held("tab%d" % a, [P, T], I32) for a in range(PASSES)]
+        load_words(tab[0], tab_words[0])
         for q in range(QUADS):
             nc.sync.dma_start(
                 out=w2_plane_raw[32 * q : 32 * q + 4, :].bitcast(I32).rearrange("r (a n) -> r a n", a=PASSES),
                 in_=w2_scales[:, 4 * q : 4 * q + 4, :].rearrange("a r n -> r a n").bitcast(I32),
             )
         load_words(tab[1], tab_words[1])
-        offs2_t = load_list("offs2_t", offs2)
-        b2_t = held("b2_t", [P, PACK], F32)
-        nc.sync.dma_start(out=b2_t[:], in_=b2.rearrange("(p t) -> p t", t=PACK))
+        w1_raw = [held("w1_raw%d" % a, [P, PACK, H], F32) for a in range(PASSES)]
+        nc.sync.dma_start(out=w1_raw[0][:], in_=w1[0:512, :].rearrange("(p j) c -> p j c", j=PACK))
+        b2_t = load_column("b2_t", b2)
         nc.sync.dma_start(out=w1_raw[1][:], in_=w1[512:1024, :].rearrange("(p j) c -> p j c", j=PACK))
+        b1_t = load_column("b1_t", b1)
+        gain_t = load_column("gain_t", gain)
         load_plane(tab2_plane, tab2_scales[0])
-        gain_t = held("gain_t", [P, PACK], F32)
-        nc.sync.dma_start(out=gain_t[:], in_=gain.rearrange("(p t) -> p t", t=PACK))
         tab2 = held("tab2", [P, T3], I32)
         load_words(tab2, tab2_words[0])
-        b1_t = held("b1_t", [P, PACK], F32)
-        nc.sync.dma_start(out=b1_t[:], in_=b1.rearrange("(p t) -> p t", t=PACK))
         w3_raw = held("w3_raw", [P, PACK, S2], F32)
         nc.sync.dma_start(out=w3_raw[:], in_=w3.rearrange("(p j) c -> p j c", j=PACK))
         w4 = held("w4", [P, S2], I32)
@@ -104,20 +116,10 @@ def tile_list_framework_pore_scores_kernel(
         load_plane(w4_plane, w4_scales[0])
         pos1_t = load_list("pos1_t", pos1)
         pos2_t = load_list("pos2_t", pos2)
-        steep_t = held("steep_t", [P, MT], F32)
-        share_t = held("share_t", [P, MT], F32)
-        lam_t = held("lam_t", [P, MT], F32)
-        with nc.allow_non_contiguous_dma(reason="one value for each output row"):
-            for dst, src in ((steep_t, steep), (share_t, share), (lam_t, lam)):
-                nc.sync.dma_start(out=dst[:], in_=src.rearrange("(t p) -> p t", p=P))
 
-        for q in range(QUADS):
-            rows = slice(32 * q, 32 * q + 8)
-            nc.vector.tensor_copy(out=tab_plane[rows, :].bitcast(I32), in_=tab_rows[rows, :])
         v_plane0 = held("v_plane0", [P, S], U8)
         nc.vector.tensor_copy(out=v_plane0[:], in_=tab_plane[:].indirect(offs_t[:]))
-        for q in range(QUADS):
-            nc.scalar.dma_start(out=v_plane1[32 * q : 32 * q + 4, :].bitcast(I32), in_=v_plane0[32 * q + 4 : 32 * q + 8, :].bitcast(I32))
+        nc.gpsimd.dma_start(out=v_plane1[0:100, :].bitcast(I32), in_=v_plane0[4:104, :].bitcast(I32))
         v_plane = [v_plane0, v_plane1]
         v = [[held("v%d_%d" % (a, u), [P, N], I32) for u in range(HALVES)] for a in range(PASSES)]
 
@@ -128,7 +130,7 @@ def tile_list_framework_pore_scores_kernel(
         gather_v(0)
 
         w2 = held("w2", [P, PASSES, 2 * H], U8)
-        nc.scalar.copy(
+        nc.vector.tensor_copy(
             out=w2[:].bitcast(U16).rearrange("p a (t m) -> p a t m", t=PACK),
             in_=w2_both[:].bitcast(U16).rearrange("p a (m t) -> p a t m", t=PACK),
         )
@@ -146,69 +148,70 @@ def tile_list_framework_pore_scores_kernel(
             )
             return grouped
 
-        w1_grouped0 = group_w1(0, nc.scalar.copy)
-        v2_plane = held("v2_plane", [P, S2], U8)
-        nc.vector.tensor_copy(out=v2_plane[:], in_=tab2_plane[:].indirect(offs2_t[:]))
         gather_v(1)
-        w1q = [quantize("w1q0", w1_grouped0)]
+        w1_grouped = [group_w1(0, nc.vector.tensor_copy)]
 
         bent = [held("bent%d" % u, [P, PACK, N], F32) for u in range(HALVES)]
         for u in range(HALVES):
-            for t in range(PACK):
-                acc = psum.tile([P, N], F32, name="acc")
-                for a in range(PASSES):
-                    mm(acc[:], w2[:, a, 256 * t : 256 * (t + 1)], w2_plane[:, a * H + P * t : a * H + P * (t + 1)],
+            accs = [bank(PACK * u + t) for t in range(PACK)]
+            for a in range(PASSES):
+                for t in range(PACK):
+                    mm(accs[t][:], w2[:, a, 256 * t : 256 * (t + 1)], w2_plane[:, a * H + P * t : a * H + P * (t + 1)],
                        v[a][u][:], v_plane[a][:, N * u : N * (u + 1)], a == 0, a == PASSES - 1, FP4X4)
-                nc.scalar.activation(out=bent[u][:, t, :], in_=acc[:], func=ACT.Gelu_apprx_tanh, bias=b2_t[:, t : t + 1])
+            for t in range(PACK):
+                nc.scalar.activation(out=bent[u][:, t, :], in_=accs[t][:], func=ACT.Gelu_apprx_tanh, bias=b2_t[:, t : t + 1])
 
-        w1q.append(quantize("w1q1", group_w1(1, nc.vector.tensor_copy)))
-
-        lin = [held("lin%d" % u, [P, PACK, N], BF16) for u in range(HALVES)]
+        w1_grouped.append(group_w1(1, nc.vector.tensor_copy))
+        w1q = [quantize("w1q%d" % a, w1_grouped[a]) for a in range(PASSES)]
+        v2_plane = held("v2_plane", [P, S2], U8)
+        nc.vector.tensor_copy(out=v2_plane[:], in_=tab2_plane[:].indirect(offs2_t[:]))
 
         def linear(u):
-            for t in range(PACK):
-                acc = psum.tile([P, N], F32, name="acc")
-                for a in range(PASSES):
-                    mm(acc[:], w1q[a][0][:, P * t : P * (t + 1)], w1q[a][1][:, P * t : P * (t + 1)],
-                       v[a][u][:], v_plane[a][:, N * u : N * (u + 1)], a == 0, a == PASSES - 1)
-                nc.scalar.activation(out=lin[u][:, t, :], in_=acc[:], func=ACT.Identity, bias=b1_t[:, t : t + 1])
-
-        def group_g(u):
-            grouped = held("g_grouped%d" % u, [P, PACK * N], BF16)
-            nc.vector.tensor_tensor(
-                out=grouped[:].rearrange("p (c i t) -> p c t i", i=4, t=PACK),
-                in0=bent[u][:].rearrange("p t (c i) -> p c t i", i=4),
-                in1=gain_t[:].unsqueeze(1).unsqueeze(3).to_broadcast([P, N // 4, PACK, 4]),
-                op=ALU.mult,
-            )
-            return grouped
-
-        def group_h(u):
             grouped = held("h_grouped%d" % u, [P, PACK * N], BF16)
-            nc.vector.tensor_copy(
+            for c in range(PACK):
+                acc = bank(PACK * u + c)
+                tokens = slice(P * c, P * (c + 1))
+                for t in range(PACK):
+                    for a in range(PASSES):
+                        mm(acc[:, P * t : P * (t + 1)], w1q[a][0][:, P * t : P * (t + 1)], w1q[a][1][:, P * t : P * (t + 1)],
+                           v[a][u][:, tokens], v_plane[a][:, N * u + P * c : N * u + P * (c + 1)], a == 0, a == PASSES - 1)
+                nc.vector.tensor_tensor(
+                    out=grouped[:, N * c : N * (c + 1)].rearrange("p (n t) -> p n t", t=PACK),
+                    in0=acc[:].rearrange("p (t n) -> p n t", t=PACK),
+                    in1=b1_t[:].unsqueeze(1).to_broadcast([P, P, PACK]),
+                    op=ALU.add,
+                )
+            return grouped
+
+        def group_g(u, copy):
+            rows = held("g_rows%d" % u, [P, PACK, N], BF16)
+            for t in range(PACK):
+                nc.gpsimd.tensor_scalar(out=rows[:, t, :], in0=bent[u][:, t, :], scalar1=gain_t[:, t : t + 1], scalar2=0.0, op0=ALU.mult, op1=ALU.add)
+            grouped = held("g_grouped%d" % u, [P, PACK * N], BF16)
+            copy(
                 out=grouped[:].rearrange("p (c i t) -> p c t i", i=4, t=PACK),
-                in_=lin[u][:].rearrange("p t (c i) -> p c t i", i=4),
+                in_=rows[:].rearrange("p t (c i) -> p c t i", i=4),
             )
             return grouped
 
-        linear(0)
-        g_grouped0 = group_g(0)
         v2 = held("v2", [P, S2], I32)
         nc.vector.tensor_copy(out=v2[:].bitcast(U32), in_=tab2[:].bitcast(U32).indirect(offs2_t[:]))
-        gq = [quantize("gq0", g_grouped0)]
+        h_grouped = [linear(u) for u in range(HALVES)]
+        hq = [quantize("hq%d" % u, h_grouped[u]) for u in range(HALVES)]
         w3_grouped = held("w3_grouped", [P, PACK * S2], BF16)
         nc.scalar.copy(
             out=w3_grouped[:].rearrange("p (c i j) -> p c j i", i=4, j=PACK),
             in_=w3_raw[:].rearrange("p j (c i) -> p c j i", i=4),
         )
-        linear(1)
-        h_grouped0 = group_h(0)
+        g_grouped0 = group_g(0, nc.scalar.copy)
+        g_grouped1 = group_g(1, nc.scalar.copy)
+        turned = bank(0)
+        nc.tensor.transpose(turned[:, 0:P], row_vecs[:], ident[:])
+        per_row = held("per_row", [P, 3 * MT], F32)
+        nc.vector.tensor_copy(out=per_row[:], in_=turned[:, 0 : 3 * MT])
+        steep_t, share_t, lam_t = [per_row[:, MT * i : MT * (i + 1)] for i in range(3)]
         pull = held("pull", [P, MT], F32)
-        nc.vector.scalar_tensor_tensor(out=pull[:], in0=steep_t[:], scalar=-1.0, in1=share_t[:], op0=ALU.mult, op1=ALU.mult)
-        hq = [quantize("hq0", h_grouped0)]
-        g_grouped1 = group_g(1)
-        w3q = quantize("w3q", w3_grouped)
-        gq.append(quantize("gq1", g_grouped1))
+        nc.vector.scalar_tensor_tensor(out=pull[:], in0=steep_t, scalar=-1.0, in1=share_t, op0=ALU.mult, op1=ALU.mult)
 
         tops = held("tops", [P, MT * HALVES], F32)
         shift = held("shift", [P, MT], F32)
@@ -216,47 +219,49 @@ def tile_list_framework_pore_scores_kernel(
         dm = [held("d%d" % m, [P, S], F32) for m in range(MT)]
         gates = [held("gate%d" % m, [P, NP], F32) for m in range(MT)]
 
+        weights = [held("weight%d" % m, [P, NP], F32) for m in range(MT)]
+
         def score(m, u):
             cols = slice(P * m, P * (m + 1))
-            acc = psum.tile([P, N], F32, name="acc")
+            acc = bank(MT * u + m)
             mm(acc[:], v2[:, cols], v2_plane[:, cols], hq[u][0][:], hq[u][1][:], True, True)
             nc.vector.tensor_scalar(
-                out=e[m][:, N * u : N * (u + 1)], in0=acc[:], scalar1=1.0, scalar2=None, op0=ALU.mult, op1=ALU.max,
+                out=e[m][:, N * u : N * (u + 1)], in0=acc[:], scalar1=1.0,
+                scalar2=None if u == 0 else tops[:, HALVES * m : HALVES * m + 1], op0=ALU.mult, op1=ALU.max,
                 accum_out=tops[:, HALVES * m + u : HALVES * m + u + 1],
             )
 
         def look(m):
-            nc.vector.tensor_scalar(
-                out=shift[:, m : m + 1], in0=tops[:, HALVES * m : HALVES * m + 1], scalar1=tops[:, HALVES * m + 1 : HALVES * m + 2],
-                scalar2=pull[:, m : m + 1], op0=ALU.max, op1=ALU.mult,
-            )
+            nc.vector.tensor_scalar(out=shift[:, m : m + 1], in0=tops[:, HALVES * m + 1 : HALVES * m + 2], scalar1=pull[:, m : m + 1], scalar2=None, op0=ALU.mult)
             nc.scalar.activation(out=gates[m][:], in_=e[m][:].indirect(pos1_t[:]), func=ACT.Sigmoid, bias=shift[:, m : m + 1], scale=steep_t[:, m : m + 1])
+            nc.scalar.activation(out=weights[m][:], in_=gates[m][:], func=ACT.Copy, scale=lam_t[:, m : m + 1])
 
         def reading(m, u):
             cols = slice(P * m, P * (m + 1))
-            acc = psum.tile([P, N], F32, name="acc")
+            acc = bank(MT * (1 - u) + m)
             mm(acc[:], w3q[0][:, cols], w3q[1][:, cols], hq[u][0][:], hq[u][1][:], True, False)
             mm(acc[:], w4[:, cols], w4_plane[:, cols], gq[u][0][:], gq[u][1][:], False, True)
             nc.scalar.copy(out=dm[m][:, N * u : N * (u + 1)], in_=acc[:])
 
         def finish(m):
-            weight = held("weight%d" % m, [P, NP], F32)
-            nc.vector.tensor_scalar(out=weight[:], in0=gates[m][:], scalar1=lam_t[:, m : m + 1], scalar2=None, op0=ALU.mult)
             res = held("res%d" % m, [P, NP], F32)
-            nc.vector.tensor_tensor(out=res[:], in0=dm[m][:].indirect(pos2_t[:]), in1=weight[:], op=ALU.mult)
+            nc.vector.tensor_tensor(out=res[:], in0=dm[m][:].indirect(pos2_t[:]), in1=weights[m][:], op=ALU.mult)
             nc.sync.dma_start(out=out[P * m : P * (m + 1), :], in_=res[:])
 
-        for m in range(MT):
-            reading(m, 0)
-        h_grouped1 = group_h(1)
-        score(0, 0)
-        hq.append(quantize("hq1", h_grouped1))
-        score(1, 0)
-        for m in range(MT):
-            if m >= 2:
-                score(m, 0)
+        def scores(m):
+            score(m, 0)
             score(m, 1)
             look(m)
+
+        def readings(m):
+            reading(m, 0)
             reading(m, 1)
+
         for m in range(MT):
+            scores(m)
+        gq = [quantize("gq0", g_grouped0)]
+        w3q = quantize("w3q", w3_grouped)
+        gq.append(quantize("gq1", g_grouped1))
+        for m in range(MT):
+            readings(m)
             finish(m)

@@ -24,6 +24,7 @@ PASSES = 2
 HALVES = 2
 QUADS = 4
 MT = 4
+LAM_ON_SCALAR = 2
 
 
 def tile_list_framework_pore_scores_kernel(
@@ -204,7 +205,6 @@ def tile_list_framework_pore_scores_kernel(
             in_=w3_raw[:].rearrange("p j (c i) -> p c j i", i=4),
         )
         g_grouped0 = group_g(0, nc.scalar.copy)
-        g_grouped1 = group_g(1, nc.scalar.copy)
         turned = bank(0)
         nc.tensor.transpose(turned[:, 0:P], row_vecs[:], ident[:])
         per_row = held("per_row", [P, 3 * MT], F32)
@@ -234,7 +234,8 @@ def tile_list_framework_pore_scores_kernel(
         def look(m):
             nc.vector.tensor_scalar(out=shift[:, m : m + 1], in0=tops[:, HALVES * m + 1 : HALVES * m + 2], scalar1=pull[:, m : m + 1], scalar2=None, op0=ALU.mult)
             nc.scalar.activation(out=gates[m][:], in_=e[m][:].indirect(pos1_t[:]), func=ACT.Sigmoid, bias=shift[:, m : m + 1], scale=steep_t[:, m : m + 1])
-            nc.scalar.activation(out=weights[m][:], in_=gates[m][:], func=ACT.Copy, scale=lam_t[:, m : m + 1])
+            if m < LAM_ON_SCALAR:
+                nc.scalar.activation(out=weights[m][:], in_=gates[m][:], func=ACT.Copy, scale=lam_t[:, m : m + 1])
 
         def reading(m, u):
             cols = slice(P * m, P * (m + 1))
@@ -244,6 +245,8 @@ def tile_list_framework_pore_scores_kernel(
             nc.scalar.copy(out=dm[m][:, N * u : N * (u + 1)], in_=acc[:])
 
         def finish(m):
+            if m >= LAM_ON_SCALAR:
+                nc.vector.tensor_scalar(out=weights[m][:], in0=gates[m][:], scalar1=lam_t[:, m : m + 1], scalar2=None, op0=ALU.mult)
             res = held("res%d" % m, [P, NP], F32)
             nc.vector.tensor_tensor(out=res[:], in0=dm[m][:].indirect(pos2_t[:]), in1=weights[m][:], op=ALU.mult)
             nc.sync.dma_start(out=out[P * m : P * (m + 1), :], in_=res[:])
@@ -257,11 +260,15 @@ def tile_list_framework_pore_scores_kernel(
             reading(m, 0)
             reading(m, 1)
 
-        for m in range(MT):
-            scores(m)
+        scores(0)
         gq = [quantize("gq0", g_grouped0)]
         w3q = quantize("w3q", w3_grouped)
+        g_grouped1 = group_g(1, nc.vector.tensor_copy)
+        scores(1)
         gq.append(quantize("gq1", g_grouped1))
         for m in range(MT):
             readings(m)
+            if m + 2 < MT:
+                scores(m + 2)
+        for m in range(MT):
             finish(m)

@@ -3,7 +3,7 @@ from contextlib import ExitStack
 import concourse.mybir as mybir
 from concourse.masks import make_identity
 
-K, T, S, H, T3, S2, NP = 1024, 2048, 1024, 512, 2048, 512, 512
+K, T, S, H, T3, S2, PICKED = 1024, 2048, 1024, 512, 2048, 512, 512
 FLOPS = 2 * (2 * K * H * S + 3 * H * S2 * S)
 
 F32 = mybir.dt.float32
@@ -19,12 +19,18 @@ ALU = mybir.AluOpType
 
 P = 128
 PACK = 4
+K_PASS = P * PACK
+PASSES = K // K_PASS
 N = 512
-PASSES = 2
-HALVES = 2
-QUADS = 4
-MT = 4
-LAM_ON_SCALAR = 2
+HALVES = S // N
+CHUNKS = N // P
+QUAD = 32
+QUADS = P // QUAD
+LIVE = 4
+NODE_TILES = S2 // P
+RUN = 4
+LIST_GROUP = 16
+LAM_ON_SCALAR = 1
 
 
 def tile_list_framework_pore_scores_kernel(
@@ -43,20 +49,43 @@ def tile_list_framework_pore_scores_kernel(
         def bank(b):
             return psum.tile([P, N], F32, name="bank%d" % b)
 
-        def load_words(dst, words):
-            nc.sync.dma_start(out=dst[:], in_=words.rearrange("p n i -> p (n i)").bitcast(I32))
+        def zeroed_plane(name, width):
+            plane = held(name, [P, width], U8)
+            nc.gpsimd.memset(plane[:].bitcast(I32), 0)
+            return plane
 
         def load_list(name, src):
-            t = lists.tile(list(src.shape), U16, name=name)
-            nc.sync.dma_start(t[:], src)
-            return t
+            offsets = lists.tile(list(src.shape), U16, name=name)
+            nc.sync.dma_start(offsets[:], src)
+            return offsets
 
-        def load_plane(dst, scales):
+        def load_words(name, words):
+            tile = held(name, [P, words.shape[1]], I32)
+            nc.sync.dma_start(out=tile[:], in_=words.rearrange("p n i -> p (n i)").bitcast(I32))
+            return tile
+
+        def load_plane(plane, scales):
             for q in range(QUADS):
-                nc.sync.dma_start(out=dst[32 * q : 32 * q + 4, :].bitcast(I32), in_=scales[4 * q : 4 * q + 4, :].bitcast(I32))
+                nc.sync.dma_start(
+                    out=plane[QUAD * q : QUAD * q + LIVE, :].bitcast(I32),
+                    in_=scales[LIVE * q : LIVE * (q + 1), :].bitcast(I32),
+                )
 
-        def mm(acc, lhs, lhs_s, rhs, rhs_s, start, stop, fmt=FP8X4):
-            nc.tensor.matmul_mx(out=acc, lhsT=lhs.bitcast(fmt), lhsT_scale=lhs_s, rhs=rhs.bitcast(FP8X4), rhs_scale=rhs_s, start=start, stop=stop)
+        def load_rows(name, rows):
+            tile = held(name, [P, PACK, rows.shape[1]], F32)
+            nc.sync.dma_start(out=tile[:], in_=rows.rearrange("(p j) c -> p j c", j=PACK))
+            return tile
+
+        def load_channels(name, vec):
+            tile = held(name, [P, PACK], F32)
+            nc.sync.dma_start(out=tile[:], in_=vec.rearrange("(p t) -> p t", t=PACK))
+            return tile
+
+        def mm(acc, lhs, lhs_plane, rhs, rhs_plane, start, stop, lhs_format=FP8X4):
+            nc.tensor.matmul_mx(
+                out=acc, lhsT=lhs.bitcast(lhs_format), lhsT_scale=lhs_plane,
+                rhs=rhs.bitcast(FP8X4), rhs_scale=rhs_plane, start=start, stop=stop,
+            )
 
         def quantize(name, grouped):
             codes = held(name + "_codes", [P, N], I32)
@@ -64,76 +93,80 @@ def tile_list_framework_pore_scores_kernel(
             nc.vector.quantize_mx(out=codes[:].bitcast(FP8X4), scales=plane[:], in_=grouped[:])
             return codes, plane
 
-        tab_plane = held("tab_plane", [P, T], U8)
-        nc.gpsimd.memset(tab_plane[:].bitcast(I32), 0)
-        w2_plane_raw = held("w2_plane_raw", [P, PASSES * H], U8)
-        nc.gpsimd.memset(w2_plane_raw[:].bitcast(I32), 0)
-        v_plane1 = held("v_plane1", [P, S], U8)
-        nc.gpsimd.memset(v_plane1[:].bitcast(I32), 0)
-        tab2_plane = held("tab2_plane", [P, T3], U8)
-        nc.gpsimd.memset(tab2_plane[:].bitcast(I32), 0)
-        w4_plane = held("w4_plane", [P, S2], U8)
-        nc.gpsimd.memset(w4_plane[:].bitcast(I32), 0)
+        def interleave(name, rows, copy):
+            grouped = held(name, [P, PACK * N], BF16)
+            copy(
+                out=grouped[:].rearrange("p (c i j) -> p c j i", i=RUN, j=PACK),
+                in_=rows[:].rearrange("p j (c i) -> p c j i", i=RUN),
+            )
+            return grouped
+
+        tab_plane = zeroed_plane("tab_plane", T)
+        w2_plane_raw = zeroed_plane("w2_plane_raw", PASSES * H)
+        v_plane1 = zeroed_plane("v_plane1", S)
+        tab2_plane = zeroed_plane("tab2_plane", T3)
+        w4_plane = zeroed_plane("w4_plane", S2)
 
         ident = held("ident", [P, P], F32)
         make_identity(nc, ident[:])
-        row_vecs = held("row_vecs", [P, P], F32)
-        nc.gpsimd.memset(row_vecs[:], 0.0)
-        for i, vec in enumerate((steep, share, lam)):
-            nc.gpsimd.dma_start(out=row_vecs[MT * i : MT * (i + 1), :], in_=vec.rearrange("(t p) -> t p", p=P))
-
-        def load_column(name, vec):
-            t = held(name, [P, PACK], F32)
-            nc.sync.dma_start(out=t[:], in_=vec.rearrange("(p t) -> p t", t=PACK))
-            return t
+        node_vecs = (steep, share, lam)
+        node_rows = held("node_rows", [P, P], F32)
+        nc.gpsimd.memset(node_rows[:], 0.0)
+        for i, vec in enumerate(node_vecs):
+            nc.gpsimd.dma_start(
+                out=node_rows[NODE_TILES * i : NODE_TILES * (i + 1), :], in_=vec.rearrange("(t p) -> t p", p=P)
+            )
 
         offs_t = load_list("offs_t", offs)
-        w2_both = held("w2_both", [P, PASSES, 2 * H // 4], I32)
-        nc.sync.dma_start(out=w2_both[:], in_=w2_words.rearrange("a p n -> p a n").bitcast(I32))
+        w2_raw = held("w2_raw", [P, PASSES, H // 2], I32)
+        nc.sync.dma_start(out=w2_raw[:], in_=w2_words.rearrange("a p n -> p a n").bitcast(I32))
         offs2_t = load_list("offs2_t", offs2)
         for q in range(QUADS):
-            nc.sync.dma_start(out=tab_plane[32 * q : 32 * q + 8, :].bitcast(I32), in_=tab_scales[:, 4 * q : 4 * q + 4, :].bitcast(I32))
-        tab = [held("tab%d" % a, [P, T], I32) for a in range(PASSES)]
-        load_words(tab[0], tab_words[0])
+            nc.sync.dma_start(
+                out=tab_plane[QUAD * q : QUAD * q + PASSES * LIVE, :].bitcast(I32),
+                in_=tab_scales[:, LIVE * q : LIVE * (q + 1), :].bitcast(I32),
+            )
+        tab = [load_words("tab0", tab_words[0])]
         for q in range(QUADS):
             nc.sync.dma_start(
-                out=w2_plane_raw[32 * q : 32 * q + 4, :].bitcast(I32).rearrange("r (a n) -> r a n", a=PASSES),
-                in_=w2_scales[:, 4 * q : 4 * q + 4, :].rearrange("a r n -> r a n").bitcast(I32),
+                out=w2_plane_raw[QUAD * q : QUAD * q + LIVE, :].bitcast(I32).rearrange("r (a n) -> r a n", a=PASSES),
+                in_=w2_scales[:, LIVE * q : LIVE * (q + 1), :].rearrange("a r n -> r a n").bitcast(I32),
             )
-        load_words(tab[1], tab_words[1])
-        w1_raw = [held("w1_raw%d" % a, [P, PACK, H], F32) for a in range(PASSES)]
-        nc.sync.dma_start(out=w1_raw[0][:], in_=w1[0:512, :].rearrange("(p j) c -> p j c", j=PACK))
-        b2_t = load_column("b2_t", b2)
-        nc.sync.dma_start(out=w1_raw[1][:], in_=w1[512:1024, :].rearrange("(p j) c -> p j c", j=PACK))
-        b1_t = load_column("b1_t", b1)
-        gain_t = load_column("gain_t", gain)
+        tab.append(load_words("tab1", tab_words[1]))
+        w1_raw = [load_rows("w1_raw0", w1[0:K_PASS, :])]
+        b2_t = load_channels("b2_t", b2)
+        w1_raw.append(load_rows("w1_raw1", w1[K_PASS:K, :]))
+        b1_t = load_channels("b1_t", b1)
+        gain_t = load_channels("gain_t", gain)
         load_plane(tab2_plane, tab2_scales[0])
-        tab2 = held("tab2", [P, T3], I32)
-        load_words(tab2, tab2_words[0])
-        w3_raw = held("w3_raw", [P, PACK, S2], F32)
-        nc.sync.dma_start(out=w3_raw[:], in_=w3.rearrange("(p j) c -> p j c", j=PACK))
-        w4 = held("w4", [P, S2], I32)
-        load_words(w4, w4_words[0])
+        tab2 = load_words("tab2", tab2_words[0])
+        w3_raw = load_rows("w3_raw", w3)
+        w4 = load_words("w4", w4_words[0])
         load_plane(w4_plane, w4_scales[0])
         pos1_t = load_list("pos1_t", pos1)
         pos2_t = load_list("pos2_t", pos2)
 
         v_plane0 = held("v_plane0", [P, S], U8)
         nc.vector.tensor_copy(out=v_plane0[:], in_=tab_plane[:].indirect(offs_t[:]))
-        nc.gpsimd.dma_start(out=v_plane1[0:100, :].bitcast(I32), in_=v_plane0[4:104, :].bitcast(I32))
+        span = QUAD * (QUADS - 1) + LIVE
+        nc.gpsimd.dma_start(out=v_plane1[0:span, :].bitcast(I32), in_=v_plane0[LIVE : LIVE + span, :].bitcast(I32))
         v_plane = [v_plane0, v_plane1]
         v = [[held("v%d_%d" % (a, u), [P, N], I32) for u in range(HALVES)] for a in range(PASSES)]
 
         def gather_v(a):
+            columns = N // LIST_GROUP
             for u in range(HALVES):
-                nc.vector.tensor_copy(out=v[a][u][:].bitcast(U32), in_=tab[a][:].bitcast(U32).indirect(offs_t[:, 32 * u : 32 * (u + 1)]))
+                window = tab[a][:].bitcast(U32)
+                nc.vector.tensor_copy(
+                    out=v[a][u][:].bitcast(U32), in_=window.indirect(offs_t[:, columns * u : columns * (u + 1)])
+                )
 
         gather_v(0)
 
         w2 = held("w2", [P, PASSES, 2 * H], U8)
         nc.vector.tensor_copy(
             out=w2[:].bitcast(U16).rearrange("p a (t m) -> p a t m", t=PACK),
-            in_=w2_both[:].bitcast(U16).rearrange("p a (m t) -> p a t m", t=PACK),
+            in_=w2_raw[:].bitcast(U16).rearrange("p a (m t) -> p a t m", t=PACK),
         )
         w2_plane = held("w2_plane", [P, PASSES * H], U8)
         nc.vector.tensor_copy(
@@ -141,41 +174,48 @@ def tile_list_framework_pore_scores_kernel(
             in_=w2_plane_raw[:].rearrange("p (a m t) -> p a t m", a=PASSES, t=PACK),
         )
 
-        def group_w1(a, copy):
+        def deal_w1(a):
             grouped = held("w1_grouped%d" % a, [P, PACK * H], BF16)
-            copy(
+            nc.vector.tensor_copy(
                 out=grouped[:].rearrange("p (t m j) -> p m j t", t=PACK, j=PACK),
                 in_=w1_raw[a][:].rearrange("p j (m t) -> p m j t", t=PACK),
             )
             return grouped
 
         gather_v(1)
-        w1_grouped = [group_w1(0, nc.vector.tensor_copy)]
+        w1_grouped = [deal_w1(0)]
 
         bent = [held("bent%d" % u, [P, PACK, N], F32) for u in range(HALVES)]
         for u in range(HALVES):
             accs = [bank(PACK * u + t) for t in range(PACK)]
             for a in range(PASSES):
                 for t in range(PACK):
-                    mm(accs[t][:], w2[:, a, 256 * t : 256 * (t + 1)], w2_plane[:, a * H + P * t : a * H + P * (t + 1)],
-                       v[a][u][:], v_plane[a][:, N * u : N * (u + 1)], a == 0, a == PASSES - 1, FP4X4)
+                    mm(
+                        accs[t][:], w2[:, a, 2 * P * t : 2 * P * (t + 1)], w2_plane[:, a * H + P * t : a * H + P * (t + 1)],
+                        v[a][u][:], v_plane[a][:, N * u : N * (u + 1)], a == 0, a == PASSES - 1, FP4X4,
+                    )
             for t in range(PACK):
-                nc.scalar.activation(out=bent[u][:, t, :], in_=accs[t][:], func=ACT.Gelu_apprx_tanh, bias=b2_t[:, t : t + 1])
+                nc.scalar.activation(
+                    out=bent[u][:, t, :], in_=accs[t][:], func=ACT.Gelu_apprx_tanh, bias=b2_t[:, t : t + 1]
+                )
 
-        w1_grouped.append(group_w1(1, nc.vector.tensor_copy))
+        w1_grouped.append(deal_w1(1))
         w1q = [quantize("w1q%d" % a, w1_grouped[a]) for a in range(PASSES)]
         v2_plane = held("v2_plane", [P, S2], U8)
         nc.vector.tensor_copy(out=v2_plane[:], in_=tab2_plane[:].indirect(offs2_t[:]))
 
-        def linear(u):
+        def linear_view(u):
             grouped = held("h_grouped%d" % u, [P, PACK * N], BF16)
-            for c in range(PACK):
-                acc = bank(PACK * u + c)
-                tokens = slice(P * c, P * (c + 1))
+            for c in range(CHUNKS):
+                acc = bank(CHUNKS * u + c)
                 for t in range(PACK):
+                    places = slice(P * t, P * (t + 1))
                     for a in range(PASSES):
-                        mm(acc[:, P * t : P * (t + 1)], w1q[a][0][:, P * t : P * (t + 1)], w1q[a][1][:, P * t : P * (t + 1)],
-                           v[a][u][:, tokens], v_plane[a][:, N * u + P * c : N * u + P * (c + 1)], a == 0, a == PASSES - 1)
+                        mm(
+                            acc[:, places], w1q[a][0][:, places], w1q[a][1][:, places],
+                            v[a][u][:, P * c : P * (c + 1)], v_plane[a][:, N * u + P * c : N * u + P * (c + 1)],
+                            a == 0, a == PASSES - 1,
+                        )
                 nc.vector.tensor_tensor(
                     out=grouped[:, N * c : N * (c + 1)].rearrange("p (n t) -> p n t", t=PACK),
                     in0=acc[:].rearrange("p (t n) -> p n t", t=PACK),
@@ -184,91 +224,85 @@ def tile_list_framework_pore_scores_kernel(
                 )
             return grouped
 
-        def group_g(u, copy):
+        def bent_view(u):
             rows = held("g_rows%d" % u, [P, PACK, N], BF16)
             for t in range(PACK):
-                nc.gpsimd.tensor_scalar(out=rows[:, t, :], in0=bent[u][:, t, :], scalar1=gain_t[:, t : t + 1], scalar2=0.0, op0=ALU.mult, op1=ALU.add)
-            grouped = held("g_grouped%d" % u, [P, PACK * N], BF16)
-            copy(
-                out=grouped[:].rearrange("p (c i t) -> p c t i", i=4, t=PACK),
-                in_=rows[:].rearrange("p t (c i) -> p c t i", i=4),
-            )
-            return grouped
+                nc.gpsimd.tensor_scalar(
+                    out=rows[:, t, :], in0=bent[u][:, t, :], scalar1=gain_t[:, t : t + 1], scalar2=0.0,
+                    op0=ALU.mult, op1=ALU.add,
+                )
+            return interleave("g_grouped%d" % u, rows, nc.scalar.copy)
 
         v2 = held("v2", [P, S2], I32)
         nc.vector.tensor_copy(out=v2[:].bitcast(U32), in_=tab2[:].bitcast(U32).indirect(offs2_t[:]))
-        h_grouped = [linear(u) for u in range(HALVES)]
+        h_grouped = [linear_view(u) for u in range(HALVES)]
         hq = [quantize("hq%d" % u, h_grouped[u]) for u in range(HALVES)]
-        w3_grouped = held("w3_grouped", [P, PACK * S2], BF16)
-        nc.scalar.copy(
-            out=w3_grouped[:].rearrange("p (c i j) -> p c j i", i=4, j=PACK),
-            in_=w3_raw[:].rearrange("p j (c i) -> p c j i", i=4),
-        )
-        g_grouped0 = group_g(0, nc.scalar.copy)
+        w3_grouped = interleave("w3_grouped", w3_raw, nc.scalar.copy)
+        g_grouped = [bent_view(u) for u in range(HALVES)]
+
         turned = bank(0)
-        nc.tensor.transpose(turned[:, 0:P], row_vecs[:], ident[:])
-        per_row = held("per_row", [P, 3 * MT], F32)
-        nc.vector.tensor_copy(out=per_row[:], in_=turned[:, 0 : 3 * MT])
-        steep_t, share_t, lam_t = [per_row[:, MT * i : MT * (i + 1)] for i in range(3)]
-        pull = held("pull", [P, MT], F32)
+        nc.tensor.transpose(turned[:, 0:P], node_rows[:], ident[:])
+        per_node = held("per_node", [P, len(node_vecs) * NODE_TILES], F32)
+        nc.vector.tensor_copy(out=per_node[:], in_=turned[:, 0 : len(node_vecs) * NODE_TILES])
+        steep_t, share_t, lam_t = [per_node[:, NODE_TILES * i : NODE_TILES * (i + 1)] for i in range(len(node_vecs))]
+        pull = held("pull", [P, NODE_TILES], F32)
         nc.vector.scalar_tensor_tensor(out=pull[:], in0=steep_t, scalar=-1.0, in1=share_t, op0=ALU.mult, op1=ALU.mult)
 
-        tops = held("tops", [P, MT * HALVES], F32)
-        shift = held("shift", [P, MT], F32)
-        e = [held("e%d" % m, [P, S], F32) for m in range(MT)]
-        dm = [held("d%d" % m, [P, S], F32) for m in range(MT)]
-        gates = [held("gate%d" % m, [P, NP], F32) for m in range(MT)]
+        tops = held("tops", [P, NODE_TILES * HALVES], F32)
+        shift = held("shift", [P, NODE_TILES], F32)
+        e = [held("e%d" % m, [P, S], F32) for m in range(NODE_TILES)]
+        d = [held("d%d" % m, [P, S], F32) for m in range(NODE_TILES)]
+        gates = [held("gate%d" % m, [P, PICKED], F32) for m in range(NODE_TILES)]
+        weights = [held("weight%d" % m, [P, PICKED], F32) for m in range(NODE_TILES)]
 
-        weights = [held("weight%d" % m, [P, NP], F32) for m in range(MT)]
-
-        def score(m, u):
-            cols = slice(P * m, P * (m + 1))
-            acc = bank(MT * u + m)
-            mm(acc[:], v2[:, cols], v2_plane[:, cols], hq[u][0][:], hq[u][1][:], True, True)
+        def scores(m):
+            nodes = slice(P * m, P * (m + 1))
+            for u in range(HALVES):
+                acc = bank(NODE_TILES * u + m)
+                mm(acc[:], v2[:, nodes], v2_plane[:, nodes], hq[u][0][:], hq[u][1][:], True, True)
+                top = HALVES * m + u
+                nc.vector.tensor_scalar(
+                    out=e[m][:, N * u : N * (u + 1)], in0=acc[:], scalar1=1.0,
+                    scalar2=None if u == 0 else tops[:, top - 1 : top], op0=ALU.mult, op1=ALU.max,
+                    accum_out=tops[:, top : top + 1],
+                )
             nc.vector.tensor_scalar(
-                out=e[m][:, N * u : N * (u + 1)], in0=acc[:], scalar1=1.0,
-                scalar2=None if u == 0 else tops[:, HALVES * m : HALVES * m + 1], op0=ALU.mult, op1=ALU.max,
-                accum_out=tops[:, HALVES * m + u : HALVES * m + u + 1],
+                out=shift[:, m : m + 1], in0=tops[:, HALVES * (m + 1) - 1 : HALVES * (m + 1)],
+                scalar1=pull[:, m : m + 1], scalar2=None, op0=ALU.mult,
             )
-
-        def look(m):
-            nc.vector.tensor_scalar(out=shift[:, m : m + 1], in0=tops[:, HALVES * m + 1 : HALVES * m + 2], scalar1=pull[:, m : m + 1], scalar2=None, op0=ALU.mult)
-            nc.scalar.activation(out=gates[m][:], in_=e[m][:].indirect(pos1_t[:]), func=ACT.Sigmoid, bias=shift[:, m : m + 1], scale=steep_t[:, m : m + 1])
+            nc.scalar.activation(
+                out=gates[m][:], in_=e[m][:].indirect(pos1_t[:]), func=ACT.Sigmoid,
+                bias=shift[:, m : m + 1], scale=steep_t[:, m : m + 1],
+            )
             if m < LAM_ON_SCALAR:
                 nc.scalar.activation(out=weights[m][:], in_=gates[m][:], func=ACT.Copy, scale=lam_t[:, m : m + 1])
 
-        def reading(m, u):
-            cols = slice(P * m, P * (m + 1))
-            acc = bank(MT * (1 - u) + m)
-            mm(acc[:], w3q[0][:, cols], w3q[1][:, cols], hq[u][0][:], hq[u][1][:], True, False)
-            mm(acc[:], w4[:, cols], w4_plane[:, cols], gq[u][0][:], gq[u][1][:], False, True)
-            nc.scalar.copy(out=dm[m][:, N * u : N * (u + 1)], in_=acc[:])
+        def readings(m):
+            nodes = slice(P * m, P * (m + 1))
+            for u in range(HALVES):
+                acc = bank(NODE_TILES * (HALVES - 1 - u) + m)
+                mm(acc[:], w3q[0][:, nodes], w3q[1][:, nodes], hq[u][0][:], hq[u][1][:], True, False)
+                mm(acc[:], w4[:, nodes], w4_plane[:, nodes], gq[u][0][:], gq[u][1][:], False, True)
+                nc.scalar.copy(out=d[m][:, N * u : N * (u + 1)], in_=acc[:])
 
         def finish(m):
             if m >= LAM_ON_SCALAR:
-                nc.vector.tensor_scalar(out=weights[m][:], in0=gates[m][:], scalar1=lam_t[:, m : m + 1], scalar2=None, op0=ALU.mult)
-            res = held("res%d" % m, [P, NP], F32)
-            nc.vector.tensor_tensor(out=res[:], in0=dm[m][:].indirect(pos2_t[:]), in1=weights[m][:], op=ALU.mult)
+                nc.vector.tensor_scalar(
+                    out=weights[m][:], in0=gates[m][:], scalar1=lam_t[:, m : m + 1], scalar2=None, op0=ALU.mult
+                )
+            res = held("res%d" % m, [P, PICKED], F32)
+            nc.vector.tensor_tensor(out=res[:], in0=d[m][:].indirect(pos2_t[:]), in1=weights[m][:], op=ALU.mult)
             nc.sync.dma_start(out=out[P * m : P * (m + 1), :], in_=res[:])
 
-        def scores(m):
-            score(m, 0)
-            score(m, 1)
-            look(m)
-
-        def readings(m):
-            reading(m, 0)
-            reading(m, 1)
-
+        ahead = 2
         scores(0)
-        gq = [quantize("gq0", g_grouped0)]
+        gq = [quantize("gq0", g_grouped[0])]
         w3q = quantize("w3q", w3_grouped)
-        g_grouped1 = group_g(1, nc.vector.tensor_copy)
         scores(1)
-        gq.append(quantize("gq1", g_grouped1))
-        for m in range(MT):
+        gq.append(quantize("gq1", g_grouped[1]))
+        for m in range(NODE_TILES):
             readings(m)
-            if m + 2 < MT:
-                scores(m + 2)
-        for m in range(MT):
+            if m + ahead < NODE_TILES:
+                scores(m + ahead)
+        for m in range(NODE_TILES):
             finish(m)

from contextlib import ExitStack

import concourse.mybir as mybir
from concourse.masks import make_identity

K, T, S, H, T3, S2, PICKED = 1024, 2048, 1024, 512, 2048, 512, 512
FLOPS = 2 * (2 * K * H * S + 3 * H * S2 * S)

F32 = mybir.dt.float32
BF16 = mybir.dt.bfloat16
I32 = mybir.dt.int32
U32 = mybir.dt.uint32
U16 = mybir.dt.uint16
U8 = mybir.dt.uint8
FP8X4 = mybir.dt.float8_e4m3fn_x4
FP4X4 = mybir.dt.float4_e2m1fn_x4
ACT = mybir.ActivationFunctionType
ALU = mybir.AluOpType

P = 128
PACK = 4
K_PASS = P * PACK
PASSES = K // K_PASS
N = 512
HALVES = S // N
CHUNKS = N // P
QUAD = 32
QUADS = P // QUAD
LIVE = 4
NODE_TILES = S2 // P
RUN = 4
LIST_GROUP = 16
LAM_ON_SCALAR = 1


def tile_list_framework_pore_scores_kernel(
    tc, tab_words, tab_scales, offs, tab2_words, tab2_scales, offs2, pos1, pos2,
    w1, b1, w2_words, w2_scales, b2, gain, w3, w4_words, w4_scales, steep, share, lam, out,
):
    nc = tc.nc
    with ExitStack() as ctx:
        lists = ctx.enter_context(tc.tile_pool(name="lists", bufs=1))
        keep = ctx.enter_context(tc.tile_pool(name="keep", bufs=1))
        psum = ctx.enter_context(tc.psum_pool(name="psum", bufs=1))

        def held(name, shape, dtype):
            return keep.tile(shape, dtype, name=name, align_bytes=64)

        def bank(b):
            return psum.tile([P, N], F32, name="bank%d" % b)

        def zeroed_plane(name, width):
            plane = held(name, [P, width], U8)
            nc.gpsimd.memset(plane[:].bitcast(I32), 0)
            return plane

        def load_list(name, src):
            offsets = lists.tile(list(src.shape), U16, name=name)
            nc.sync.dma_start(offsets[:], src)
            return offsets

        def load_words(name, words):
            tile = held(name, [P, words.shape[1]], I32)
            nc.sync.dma_start(out=tile[:], in_=words.rearrange("p n i -> p (n i)").bitcast(I32))
            return tile

        def load_plane(plane, scales):
            for q in range(QUADS):
                nc.sync.dma_start(
                    out=plane[QUAD * q : QUAD * q + LIVE, :].bitcast(I32),
                    in_=scales[LIVE * q : LIVE * (q + 1), :].bitcast(I32),
                )

        def load_rows(name, rows):
            tile = held(name, [P, PACK, rows.shape[1]], F32)
            nc.sync.dma_start(out=tile[:], in_=rows.rearrange("(p j) c -> p j c", j=PACK))
            return tile

        def load_channels(name, vec):
            tile = held(name, [P, PACK], F32)
            nc.sync.dma_start(out=tile[:], in_=vec.rearrange("(p t) -> p t", t=PACK))
            return tile

        def mm(acc, lhs, lhs_plane, rhs, rhs_plane, start, stop, lhs_format=FP8X4):
            nc.tensor.matmul_mx(
                out=acc, lhsT=lhs.bitcast(lhs_format), lhsT_scale=lhs_plane,
                rhs=rhs.bitcast(FP8X4), rhs_scale=rhs_plane, start=start, stop=stop,
            )

        def quantize(name, grouped):
            codes = held(name + "_codes", [P, N], I32)
            plane = held(name + "_plane", [P, N], U8)
            nc.vector.quantize_mx(out=codes[:].bitcast(FP8X4), scales=plane[:], in_=grouped[:])
            return codes, plane

        def interleave(name, rows, copy):
            grouped = held(name, [P, PACK * N], BF16)
            copy(
                out=grouped[:].rearrange("p (c i j) -> p c j i", i=RUN, j=PACK),
                in_=rows[:].rearrange("p j (c i) -> p c j i", i=RUN),
            )
            return grouped

        tab_plane = zeroed_plane("tab_plane", T)
        w2_plane_raw = zeroed_plane("w2_plane_raw", PASSES * H)
        v_plane1 = zeroed_plane("v_plane1", S)
        tab2_plane = zeroed_plane("tab2_plane", T3)
        w4_plane = zeroed_plane("w4_plane", S2)

        ident = held("ident", [P, P], F32)
        make_identity(nc, ident[:])
        node_vecs = (steep, share, lam)
        node_rows = held("node_rows", [P, P], F32)
        nc.gpsimd.memset(node_rows[:], 0.0)
        for i, vec in enumerate(node_vecs):
            nc.gpsimd.dma_start(
                out=node_rows[NODE_TILES * i : NODE_TILES * (i + 1), :], in_=vec.rearrange("(t p) -> t p", p=P)
            )

        offs_t = load_list("offs_t", offs)
        w2_raw = held("w2_raw", [P, PASSES, H // 2], I32)
        nc.sync.dma_start(out=w2_raw[:], in_=w2_words.rearrange("a p n -> p a n").bitcast(I32))
        offs2_t = load_list("offs2_t", offs2)
        for q in range(QUADS):
            nc.sync.dma_start(
                out=tab_plane[QUAD * q : QUAD * q + PASSES * LIVE, :].bitcast(I32),
                in_=tab_scales[:, LIVE * q : LIVE * (q + 1), :].bitcast(I32),
            )
        tab = [load_words("tab0", tab_words[0])]
        for q in range(QUADS):
            nc.sync.dma_start(
                out=w2_plane_raw[QUAD * q : QUAD * q + LIVE, :].bitcast(I32).rearrange("r (a n) -> r a n", a=PASSES),
                in_=w2_scales[:, LIVE * q : LIVE * (q + 1), :].rearrange("a r n -> r a n").bitcast(I32),
            )
        tab.append(load_words("tab1", tab_words[1]))
        w1_raw = [load_rows("w1_raw0", w1[0:K_PASS, :])]
        b2_t = load_channels("b2_t", b2)
        w1_raw.append(load_rows("w1_raw1", w1[K_PASS:K, :]))
        b1_t = load_channels("b1_t", b1)
        gain_t = load_channels("gain_t", gain)
        load_plane(tab2_plane, tab2_scales[0])
        tab2 = load_words("tab2", tab2_words[0])
        w3_raw = load_rows("w3_raw", w3)
        w4 = load_words("w4", w4_words[0])
        load_plane(w4_plane, w4_scales[0])
        pos1_t = load_list("pos1_t", pos1)
        pos2_t = load_list("pos2_t", pos2)

        v_plane0 = held("v_plane0", [P, S], U8)
        nc.vector.tensor_copy(out=v_plane0[:], in_=tab_plane[:].indirect(offs_t[:]))
        span = QUAD * (QUADS - 1) + LIVE
        nc.gpsimd.dma_start(out=v_plane1[0:span, :].bitcast(I32), in_=v_plane0[LIVE : LIVE + span, :].bitcast(I32))
        v_plane = [v_plane0, v_plane1]
        v = [[held("v%d_%d" % (a, u), [P, N], I32) for u in range(HALVES)] for a in range(PASSES)]

        def gather_v(a):
            columns = N // LIST_GROUP
            for u in range(HALVES):
                window = tab[a][:].bitcast(U32)
                nc.vector.tensor_copy(
                    out=v[a][u][:].bitcast(U32), in_=window.indirect(offs_t[:, columns * u : columns * (u + 1)])
                )

        gather_v(0)

        w2 = held("w2", [P, PASSES, 2 * H], U8)
        nc.vector.tensor_copy(
            out=w2[:].bitcast(U16).rearrange("p a (t m) -> p a t m", t=PACK),
            in_=w2_raw[:].bitcast(U16).rearrange("p a (m t) -> p a t m", t=PACK),
        )
        w2_plane = held("w2_plane", [P, PASSES * H], U8)
        nc.vector.tensor_copy(
            out=w2_plane[:].rearrange("p (a t m) -> p a t m", a=PASSES, t=PACK),
            in_=w2_plane_raw[:].rearrange("p (a m t) -> p a t m", a=PASSES, t=PACK),
        )

        def deal_w1(a):
            grouped = held("w1_grouped%d" % a, [P, PACK * H], BF16)
            nc.vector.tensor_copy(
                out=grouped[:].rearrange("p (t m j) -> p m j t", t=PACK, j=PACK),
                in_=w1_raw[a][:].rearrange("p j (m t) -> p m j t", t=PACK),
            )
            return grouped

        gather_v(1)
        w1_grouped = [deal_w1(0)]

        bent = [held("bent%d" % u, [P, PACK, N], F32) for u in range(HALVES)]
        for u in range(HALVES):
            accs = [bank(PACK * u + t) for t in range(PACK)]
            for a in range(PASSES):
                for t in range(PACK):
                    mm(
                        accs[t][:], w2[:, a, 2 * P * t : 2 * P * (t + 1)], w2_plane[:, a * H + P * t : a * H + P * (t + 1)],
                        v[a][u][:], v_plane[a][:, N * u : N * (u + 1)], a == 0, a == PASSES - 1, FP4X4,
                    )
            for t in range(PACK):
                nc.scalar.activation(
                    out=bent[u][:, t, :], in_=accs[t][:], func=ACT.Gelu_apprx_tanh, bias=b2_t[:, t : t + 1]
                )

        w1_grouped.append(deal_w1(1))
        w1q = [quantize("w1q%d" % a, w1_grouped[a]) for a in range(PASSES)]
        v2_plane = held("v2_plane", [P, S2], U8)
        nc.vector.tensor_copy(out=v2_plane[:], in_=tab2_plane[:].indirect(offs2_t[:]))

        def linear_view(u):
            grouped = held("h_grouped%d" % u, [P, PACK * N], BF16)
            for c in range(CHUNKS):
                acc = bank(CHUNKS * u + c)
                for t in range(PACK):
                    places = slice(P * t, P * (t + 1))
                    for a in range(PASSES):
                        mm(
                            acc[:, places], w1q[a][0][:, places], w1q[a][1][:, places],
                            v[a][u][:, P * c : P * (c + 1)], v_plane[a][:, N * u + P * c : N * u + P * (c + 1)],
                            a == 0, a == PASSES - 1,
                        )
                nc.vector.tensor_tensor(
                    out=grouped[:, N * c : N * (c + 1)].rearrange("p (n t) -> p n t", t=PACK),
                    in0=acc[:].rearrange("p (t n) -> p n t", t=PACK),
                    in1=b1_t[:].unsqueeze(1).to_broadcast([P, P, PACK]),
                    op=ALU.add,
                )
            return grouped

        def bent_view(u):
            rows = held("g_rows%d" % u, [P, PACK, N], BF16)
            for t in range(PACK):
                nc.gpsimd.tensor_scalar(
                    out=rows[:, t, :], in0=bent[u][:, t, :], scalar1=gain_t[:, t : t + 1], scalar2=0.0,
                    op0=ALU.mult, op1=ALU.add,
                )
            return interleave("g_grouped%d" % u, rows, nc.scalar.copy)

        v2 = held("v2", [P, S2], I32)
        nc.vector.tensor_copy(out=v2[:].bitcast(U32), in_=tab2[:].bitcast(U32).indirect(offs2_t[:]))
        h_grouped = [linear_view(u) for u in range(HALVES)]
        hq = [quantize("hq%d" % u, h_grouped[u]) for u in range(HALVES)]
        w3_grouped = interleave("w3_grouped", w3_raw, nc.scalar.copy)
        g_grouped = [bent_view(u) for u in range(HALVES)]

        turned = bank(0)
        nc.tensor.transpose(turned[:, 0:P], node_rows[:], ident[:])
        per_node = held("per_node", [P, len(node_vecs) * NODE_TILES], F32)
        nc.vector.tensor_copy(out=per_node[:], in_=turned[:, 0 : len(node_vecs) * NODE_TILES])
        steep_t, share_t, lam_t = [per_node[:, NODE_TILES * i : NODE_TILES * (i + 1)] for i in range(len(node_vecs))]
        pull = held("pull", [P, NODE_TILES], F32)
        nc.vector.scalar_tensor_tensor(out=pull[:], in0=steep_t, scalar=-1.0, in1=share_t, op0=ALU.mult, op1=ALU.mult)

        tops = held("tops", [P, NODE_TILES * HALVES], F32)
        shift = held("shift", [P, NODE_TILES], F32)
        e = [held("e%d" % m, [P, S], F32) for m in range(NODE_TILES)]
        d = [held("d%d" % m, [P, S], F32) for m in range(NODE_TILES)]
        gates = [held("gate%d" % m, [P, PICKED], F32) for m in range(NODE_TILES)]
        weights = [held("weight%d" % m, [P, PICKED], F32) for m in range(NODE_TILES)]

        def scores(m):
            nodes = slice(P * m, P * (m + 1))
            for u in range(HALVES):
                acc = bank(NODE_TILES * u + m)
                mm(acc[:], v2[:, nodes], v2_plane[:, nodes], hq[u][0][:], hq[u][1][:], True, True)
                top = HALVES * m + u
                nc.vector.tensor_scalar(
                    out=e[m][:, N * u : N * (u + 1)], in0=acc[:], scalar1=1.0,
                    scalar2=None if u == 0 else tops[:, top - 1 : top], op0=ALU.mult, op1=ALU.max,
                    accum_out=tops[:, top : top + 1],
                )
            nc.vector.tensor_scalar(
                out=shift[:, m : m + 1], in0=tops[:, HALVES * (m + 1) - 1 : HALVES * (m + 1)],
                scalar1=pull[:, m : m + 1], scalar2=None, op0=ALU.mult,
            )
            nc.scalar.activation(
                out=gates[m][:], in_=e[m][:].indirect(pos1_t[:]), func=ACT.Sigmoid,
                bias=shift[:, m : m + 1], scale=steep_t[:, m : m + 1],
            )
            if m < LAM_ON_SCALAR:
                nc.scalar.activation(out=weights[m][:], in_=gates[m][:], func=ACT.Copy, scale=lam_t[:, m : m + 1])

        def readings(m):
            nodes = slice(P * m, P * (m + 1))
            for u in range(HALVES):
                acc = bank(NODE_TILES * (HALVES - 1 - u) + m)
                mm(acc[:], w3q[0][:, nodes], w3q[1][:, nodes], hq[u][0][:], hq[u][1][:], True, False)
                mm(acc[:], w4[:, nodes], w4_plane[:, nodes], gq[u][0][:], gq[u][1][:], False, True)
                nc.scalar.copy(out=d[m][:, N * u : N * (u + 1)], in_=acc[:])

        def finish(m):
            if m >= LAM_ON_SCALAR:
                nc.vector.tensor_scalar(
                    out=weights[m][:], in0=gates[m][:], scalar1=lam_t[:, m : m + 1], scalar2=None, op0=ALU.mult
                )
            res = held("res%d" % m, [P, PICKED], F32)
            nc.vector.tensor_tensor(out=res[:], in0=d[m][:].indirect(pos2_t[:]), in1=weights[m][:], op=ALU.mult)
            nc.sync.dma_start(out=out[P * m : P * (m + 1), :], in_=res[:])

        ahead = 2
        scores(0)
        gq = [quantize("gq0", g_grouped[0])]
        w3q = quantize("w3q", w3_grouped)
        scores(1)
        gq.append(quantize("gq1", g_grouped[1]))
        for m in range(NODE_TILES):
            readings(m)
            if m + ahead < NODE_TILES:
                scores(m + ahead)
        for m in range(NODE_TILES):
            finish(m)
